import numpy as np
import ml_dtypes


def mxq(x, axis, fmt="e4m3"):
    dtype, down = {"e4m3": (ml_dtypes.float8_e4m3fn, 7), "e5m2": (ml_dtypes.float8_e5m2, 14)}[fmt]
    v = np.moveaxis(np.asarray(x, np.float32).astype(ml_dtypes.bfloat16).astype(np.float64), axis, -1)
    blocks = v.reshape(v.shape[:-1] + (-1, 32))
    amax = np.abs(blocks).max(-1, keepdims=True)
    byte = np.maximum(np.where(amax > 0, np.frexp(amax)[1] - 1 + 127, 0) - down, 1)
    scale = np.exp2(byte - 127.0)
    codes = (blocks / scale).astype(np.float32).astype(dtype).astype(np.float64)
    return np.moveaxis((codes * scale).reshape(v.shape), -1, axis)


WIDE = False


def mx_kscale(k):
    if not WIDE:
        return np.ones(k)
    levels = np.array([10, -10, 5, -5, 0])
    if k % 512:
        return np.exp2(np.random.permutation(np.resize(levels, k // 32))).repeat(32)
    a = np.empty((k // 512, 16))
    for p in range(k // 512):
        a[p, :8] = np.random.permutation(np.resize(levels, 8))
        for g in range(8):
            far = levels[np.abs(levels - a[p, g]) >= 10]
            a[p, g + 8] = far[np.random.randint(len(far))]
    return np.exp2(a.ravel()).repeat(32)


def f64(x):
    return np.asarray(x).astype(np.float64)


def striped(idx):
    return np.tile(np.asarray(idx).reshape(-1, 16).T, (8, 1)).astype(np.uint16)


def unstriped(offs):
    return offs[:16].T.reshape(-1).astype(np.int64)


E2M1 = np.array([0.0, 0.5, 1.0, 1.5, 2.0, 3.0, 4.0, 6.0, -0.0, -0.5, -1.0, -1.5, -2.0, -3.0, -4.0, -6.0])


def pack_weight(w, fmt):
    k, n = w.shape
    w = f64(np.asarray(w, np.float32).astype(ml_dtypes.bfloat16)).reshape(k // 32, 32, n)
    amax = np.abs(w).max(1)
    if fmt == "e4m3":
        byte = np.frexp(amax)[1] - 1 + 127 - 7
    else:
        mant, ex = np.frexp(amax / 6.0)
        byte = np.where(mant > 0.5, ex, ex - 1) + 127
    byte = np.clip(np.where(amax > 0, byte, 1), 1, 254)
    scaled = (w * np.exp2(127.0 - byte)[:, None, :]).reshape(k, n).astype(np.float32)
    by_word = np.ascontiguousarray(scaled.reshape(k // 512, 128, 4, n).transpose(0, 1, 3, 2))
    if fmt == "e4m3":
        words = by_word.astype(ml_dtypes.float8_e4m3fn).view(np.uint8)
    else:
        c = by_word.astype(ml_dtypes.float4_e2m1fn).view(np.uint8) & 0xF
        words = (c[..., 0::2] | (c[..., 1::2] << 4)).reshape(k // 512, 128, 2 * n)
    return np.ascontiguousarray(words), np.ascontiguousarray(byte.astype(np.uint8).reshape(k // 512, 16, n))


def unpack_weight(words, scales, fmt):
    g, _, n = scales.shape
    words = np.ascontiguousarray(words).reshape(g, 128, n, -1)
    if fmt == "e4m3":
        vals = words.view(ml_dtypes.float8_e4m3fn).astype(np.float64)
    else:
        nib = np.empty((g, 128, n, 4), np.uint8)
        nib[..., 0::2] = words & 0xF
        nib[..., 1::2] = words >> 4
        vals = E2M1[nib]
    vals = vals * np.repeat(np.exp2(scales.astype(np.float64) - 127.0), 8, axis=1)[..., None]
    return vals.transpose(0, 1, 3, 2).reshape(g * 512, n)


K, R, F, T, J, G = 512, 128, 512, 2048, 512, 64


def setup_inputs():
    n = np.random.standard_normal
    idx = np.random.permutation(T)[:J]
    fk = mx_kscale(K)
    tabp = pack_weight(n((K, T)) / fk[:, None], "e4m3")
    dtabp = pack_weight(n((K, T)) / fk[:, None], "e4m3")
    return {
        "tab_words": tabp[0],
        "tab_scales": tabp[1],
        "dtab_words": dtabp[0],
        "dtab_scales": dtabp[1],
        "w1": (n((K, R)) * 1 / np.sqrt(K) * fk[:, None]).astype(np.float32),
        "w2": (n((K, R)) * 0.7 / np.sqrt(K) * fk[:, None]).astype(np.float32),
        "og": (np.random.uniform(0.5, 2.0, (R, 1))).astype(np.float32),
        "base": (0.3 * n((R, G))).astype(np.float32),
        "offs": striped(idx),
    }


def reference(tab_words, tab_scales, dtab_words, dtab_scales, w1, w2, og, base, offs):
    idx = unstriped(offs)
    tabu = unpack_weight(tab_words, tab_scales, "e4m3")
    dtabu = unpack_weight(dtab_words, dtab_scales, "e4m3")
    w1q = mxq(f64(w1), 0, "e4m3")
    tabidxg = tabu[:, idx]
    a = w1q.T @ tabidxg
    dtabidxg = dtabu[:, idx]
    ta = w1q.T @ dtabidxg
    w2q = mxq(f64(w2), 0, "e4m3")
    b = w2q.T @ tabidxg
    tb = w2q.T @ dtabidxg
    p = np.exp(b)
    z = p.reshape(R, G, J // G).sum(axis=2)
    n1 = (p * a).reshape(R, G, J // G).sum(axis=2)
    u1 = np.tanh(n1 / z)
    tp = tb * p
    tz = tp.reshape(R, G, J // G).sum(axis=2)
    tn1 = (tp * a + ta * p).reshape(R, G, J // G).sum(axis=2)
    tu1 = (tn1 - tz * n1 / z) / z * (1.0 - np.square(u1))
    y = tu1 * f64(og) + f64(base)
    return y

@@ -1,0 +1,165 @@
+from contextlib import ExitStack
+
+import concourse.mybir as mybir
+from concourse.masks import make_identity
+
+K, R, T, J, G = 512, 128, 2048, 512, 64
+P = 128
+PACK = 4
+U, V = 4, 2
+HALF = J // 2
+GH = G // 2
+FLOPS = 4 * 2 * K * R * J
+
+F32 = mybir.dt.float32
+BF16 = mybir.dt.bfloat16
+I32 = mybir.dt.int32
+U32 = mybir.dt.uint32
+U16 = mybir.dt.uint16
+U8 = mybir.dt.uint8
+FP8X4 = mybir.dt.float8_e4m3fn_x4
+ALU = mybir.AluOpType
+ACT = mybir.ActivationFunctionType
+AX = mybir.AxisListType
+
+
+def tile_attend_tcgatepool_kernel(tc, tab_words, tab_scales, dtab_words, dtab_scales, w1, w2, og, base, offs, out):
+    nc = tc.nc
+    with ExitStack() as ctx:
+        sb = ctx.enter_context(tc.tile_pool(name="sb", bufs=1))
+        ps = ctx.enter_context(tc.psum_pool(name="ps", bufs=1))
+
+        offsets = sb.tile([P, J // 16], U16, name="offsets")
+        nc.sync.dma_start(offsets[:], offs)
+
+        tab_sc = sb.tile([P, T], U8, name="tab_sc", align_bytes=64)
+        dtab_sc = sb.tile([P, T], U8, name="dtab_sc", align_bytes=64)
+        nc.vector.memset(tab_sc[:].bitcast(I32), 0)
+        nc.vector.memset(dtab_sc[:].bitcast(I32), 0)
+        for q in range(4):
+            nc.sync.dma_start(tab_sc[32 * q : 32 * q + 4, :].bitcast(I32), tab_scales[0, 4 * q : 4 * q + 4, :].bitcast(I32))
+
+        w2_raw = sb.tile([P, PACK, R], F32, name="w2_raw")
+        w1_raw = sb.tile([P, PACK, R], F32, name="w1_raw")
+        tab_w = sb.tile([P, T], U32, name="tab_w", align_bytes=64)
+        dtab_w = sb.tile([P, T], U32, name="dtab_w", align_bytes=64)
+        nc.sync.dma_start(w2_raw[:], w2.rearrange("(p t) r -> p t r", t=PACK))
+        nc.sync.dma_start(tab_w[:].bitcast(I32), tab_words[0].rearrange("p n t -> p (n t)").bitcast(I32))
+        nc.sync.dma_start(w1_raw[:], w1.rearrange("(p t) r -> p t r", t=PACK))
+        for q in range(4):
+            nc.sync.dma_start(dtab_sc[32 * q + 4 : 32 * q + 8, :].bitcast(I32), dtab_scales[0, 4 * q : 4 * q + 4, :].bitcast(I32))
+        nc.sync.dma_start(dtab_w[:].bitcast(I32), dtab_words[0].rearrange("p n t -> p (n t)").bitcast(I32))
+
+        ident = sb.tile([P, P], F32, name="ident")
+        make_identity(nc, ident[:])
+        warm = sb.tile([P, 1], F32, name="warm")
+        nc.scalar.activation(warm[:], ident[:, 0:1], ACT.Exp)
+        gain = sb.tile([P, 1], F32, name="gain")
+        nc.gpsimd.dma_start(gain[:], og)
+        base_sb = sb.tile([P, G], F32, name="base_sb")
+        nc.gpsimd.dma_start(base_sb[:], base)
+        neg_gain = sb.tile([P, 1], F32, name="neg_gain")
+        nc.gpsimd.tensor_scalar(neg_gain[:], gain[:], -1.0, 0.0, ALU.mult, ALU.add)
+        coef = sb.tile([P, 2, G], F32, name="coef")
+        nc.gpsimd.memset(coef[:, 1, :], 1.0)
+
+        tab_sg = sb.tile([P, J], U8, name="tab_sg", align_bytes=64)
+        dtab_sg = sb.tile([P, J], U8, name="dtab_sg", align_bytes=64)
+        nc.vector.tensor_copy(tab_sg[:], tab_sc[:].indirect(offsets[:]))
+
+        def quantise(raw, name):
+            grouped = sb.tile([P, R, PACK], BF16, name=name + "_grouped", align_bytes=64)
+            nc.scalar.copy(grouped[:], raw[:].rearrange("p t r -> p r t"))
+            codes = sb.tile([P, R], U32, name=name + "_codes", align_bytes=64)
+            scales = sb.tile([P, R], U8, name=name + "_scales", align_bytes=64)
+            nc.vector.quantize_mx(out=codes[:].bitcast(FP8X4), scales=scales[:], in_=grouped[:].rearrange("p r t -> p (r t)"))
+            return codes, scales
+
+        def product(dst, weights, words, scales):
+            nc.tensor.matmul_mx(out=dst, lhsT=weights[0][:].bitcast(FP8X4), lhsT_scale=weights[1][:],
+                                rhs=words.bitcast(FP8X4), rhs_scale=scales, start=True, stop=True)
+
+        def list_half(h):
+            return offsets[:, h * (HALF // 16) : (h + 1) * (HALF // 16)]
+
+        def by_slot(bank):
+            return bank.rearrange("p (g u v) -> p u g v", u=U, v=V)
+
+        w2q = quantise(w2_raw, "w2")
+        tab_g = [sb.tile([P, HALF], U32, name=f"tab_g{h}", align_bytes=64) for h in range(2)]
+        b = [ps.tile([P, HALF], F32, name=f"b{h}") for h in range(2)]
+        a = ps.tile([P, J], F32, name="a")
+        for h in range(2):
+            nc.vector.tensor_copy(tab_g[h][:], tab_w[:].indirect(list_half(h)))
+            product(b[h][:], w2q, tab_g[h][:], tab_sg[:, h * HALF : (h + 1) * HALF])
+        nc.vector.tensor_copy(dtab_sg[:], dtab_sc[:].indirect(offsets[:]))
+        w1q = quantise(w1_raw, "w1")
+        for h in range(2):
+            product(a[:, h * HALF : (h + 1) * HALF], w1q, tab_g[h][:], tab_sg[:, h * HALF : (h + 1) * HALF])
+
+        top = sb.tile([P, G], F32, name="top", tag="dtab_sc", align_bytes=64)
+        shifted = [sb.tile([P, U, GH, V], F32, name=f"shifted{h}") for h in range(2)]
+        pw = sb.tile([P, U, 2, G, V], F32, name="pw")
+        for h in range(2):
+            gs = slice(h * GH, (h + 1) * GH)
+            nc.vector.tensor_reduce(top[:, gs], b[h][:].rearrange("p (g i) -> p g i", i=U * V), AX.X, ALU.max)
+        for h in range(2):
+            gs = slice(h * GH, (h + 1) * GH)
+            nc.vector.tensor_tensor(shifted[h][:], by_slot(b[h][:]),
+                                    top[:, gs].unsqueeze(1).unsqueeze(3).to_broadcast([P, U, GH, V]), ALU.subtract)
+            nc.scalar.activation(pw[:, :, 0, gs, :], shifted[h][:], ACT.Exp)
+        for h in range(2):
+            gs = slice(h * GH, (h + 1) * GH)
+            nc.vector.tensor_tensor(pw[:, :, 1, gs, :], by_slot(a[:])[:, :, gs, :], pw[:, :, 0, gs, :], ALU.mult)
+
+        dtab_g = [sb.tile([P, HALF], U32, name=f"dtab_g{h}", align_bytes=64) for h in range(2)]
+        tb = ps.tile([P, J], F32, name="tb")
+        ta = ps.tile([P, J], F32, name="ta")
+        for h in range(2):
+            cols = slice(h * HALF, (h + 1) * HALF)
+            nc.vector.tensor_copy(dtab_g[h][:], dtab_w[:].indirect(list_half(h)))
+            product(tb[:, cols], w2q, dtab_g[h][:], dtab_sg[4:P, cols])
+        for h in range(2):
+            cols = slice(h * HALF, (h + 1) * HALF)
+            product(ta[:, cols], w1q, dtab_g[h][:], dtab_sg[4:P, cols])
+
+        zn = sb.tile([P, 2, G], F32, name="zn", tag="dtab_w", align_bytes=64)
+        nc.vector.tensor_reduce(zn[:], pw[:].rearrange("p u h g v -> p h g u v"), AX.XY, ALU.add)
+
+        tpw = [sb.tile([P, 2, G, V], F32, name=f"tpw{u}") for u in range(U)]
+        turned = ps.tile([P, P], F32, name="turned")
+        for u in range(U):
+            nc.vector.tensor_tensor(tpw[u][:], by_slot(tb[:])[:, u].unsqueeze(1).to_broadcast([P, 2, G, V]), pw[:, u], ALU.mult)
+            for v in range(V):
+                nc.tensor.matmul(turned[:], lhsT=tpw[u][:].rearrange("p h g v -> p (h g) v")[:, :, v], rhs=ident[:],
+                                 is_transpose=True, start=(u == 0 and v == 0), stop=(u == U - 1 and v == V - 1))
+        ta_sb = sb.tile([P, U, G, V], F32, name="ta_sb")
+        nc.scalar.copy(ta_sb[:], by_slot(ta[:]))
+        tap = sb.tile([P, U, G, V], F32, name="tap")
+        nc.gpsimd.tensor_tensor(tap[:], ta_sb[:], pw[:, :, 0], ALU.mult)
+
+        staged = sb.tile([P, P], F32, name="staged")
+        nc.scalar.copy(staged[:], turned[:])
+        tzn = ps.tile([P, 2, G], F32, name="tzn")
+        nc.tensor.transpose(tzn[:].rearrange("p h g -> p (h g)"), staged[:], ident[:])
+
+        rz = sb.tile([P, G], F32, name="rz")
+        nc.vector.reciprocal(rz[:], zn[:, 0, :])
+        nc.vector.scalar_tensor_tensor(coef[:, 0, :], zn[:, 1, :], -1.0, rz[:], ALU.mult, ALU.mult)
+        u1 = sb.tile([P, G], F32, name="u1")
+        u2 = sb.tile([P, G], F32, name="u2")
+        nc.scalar.activation(u1[:], coef[:, 0, :], ACT.Tanh)
+        nc.scalar.activation(u2[:], u1[:], ACT.Square)
+
+        terms = sb.tile([P, 3, G], F32, name="terms")
+        nc.vector.tensor_reduce(terms[:, 2, :], tap[:].rearrange("p u g v -> p g u v"), AX.XY, ALU.add)
+        nc.vector.tensor_tensor(terms[:, 0:2, :], tzn[:], coef[:], ALU.mult)
+        slope = sb.tile([P, G], F32, name="slope")
+        nc.vector.scalar_tensor_tensor(slope[:], u2[:], 1.0, rz[:], ALU.subtract, ALU.mult)
+        total = sb.tile([P, G], F32, name="total")
+        nc.vector.tensor_reduce(total[:], terms[:].rearrange("p s g -> p g s"), AX.X, ALU.add)
+        scaled = sb.tile([P, G], F32, name="scaled")
+        nc.vector.scalar_tensor_tensor(scaled[:], total[:], neg_gain[:], slope[:], ALU.mult, ALU.mult)
+        res = sb.tile([P, G], F32, name="res")
+        nc.vector.tensor_tensor(res[:], scaled[:], base_sb[:], ALU.add)
+        nc.sync.dma_start(out, res[:])

@@ -32,22 +32,22 @@ def tile_attend_tcgatepool_kernel(tc, tab_words, tab_scales, dtab_words, dtab_sc
         offsets = sb.tile([P, J // 16], U16, name="offsets")
         nc.sync.dma_start(offsets[:], offs)
 
+        w2_raw = sb.tile([P, PACK, R], F32, name="w2_raw")
+        nc.sync.dma_start(w2_raw[:], w2.rearrange("(p t) r -> p t r", t=PACK))
         tab_sc = sb.tile([P, T], U8, name="tab_sc", align_bytes=64)
         dtab_sc = sb.tile([P, T], U8, name="dtab_sc", align_bytes=64)
-        nc.vector.memset(tab_sc[:].bitcast(I32), 0)
-        nc.vector.memset(dtab_sc[:].bitcast(I32), 0)
+        nc.gpsimd.memset(tab_sc[:].bitcast(I32), 0)
+        nc.gpsimd.memset(dtab_sc[:].bitcast(I32), 0)
         for q in range(4):
             nc.sync.dma_start(tab_sc[32 * q : 32 * q + 4, :].bitcast(I32), tab_scales[0, 4 * q : 4 * q + 4, :].bitcast(I32))
 
-        w2_raw = sb.tile([P, PACK, R], F32, name="w2_raw")
         w1_raw = sb.tile([P, PACK, R], F32, name="w1_raw")
         tab_w = sb.tile([P, T], U32, name="tab_w", align_bytes=64)
         dtab_w = sb.tile([P, T], U32, name="dtab_w", align_bytes=64)
-        nc.sync.dma_start(w2_raw[:], w2.rearrange("(p t) r -> p t r", t=PACK))
         nc.sync.dma_start(tab_w[:].bitcast(I32), tab_words[0].rearrange("p n t -> p (n t)").bitcast(I32))
-        nc.sync.dma_start(w1_raw[:], w1.rearrange("(p t) r -> p t r", t=PACK))
         for q in range(4):
             nc.sync.dma_start(dtab_sc[32 * q + 4 : 32 * q + 8, :].bitcast(I32), dtab_scales[0, 4 * q : 4 * q + 4, :].bitcast(I32))
+        nc.sync.dma_start(w1_raw[:], w1.rearrange("(p t) r -> p t r", t=PACK))
         nc.sync.dma_start(dtab_w[:].bitcast(I32), dtab_words[0].rearrange("p n t -> p (n t)").bitcast(I32))
 
         ident = sb.tile([P, P], F32, name="ident")
@@ -99,7 +99,7 @@ def tile_attend_tcgatepool_kernel(tc, tab_words, tab_scales, dtab_words, dtab_sc
 
         top = sb.tile([P, G], F32, name="top", tag="dtab_sc", align_bytes=64)
         shifted = [sb.tile([P, U, GH, V], F32, name=f"shifted{h}") for h in range(2)]
-        pw = sb.tile([P, U, 2, G, V], F32, name="pw")
+        p = sb.tile([P, U, G, V], F32, name="p")
         for h in range(2):
             gs = slice(h * GH, (h + 1) * GH)
             nc.vector.tensor_reduce(top[:, gs], b[h][:].rearrange("p (g i) -> p g i", i=U * V), AX.X, ALU.max)
@@ -107,10 +107,7 @@ def tile_attend_tcgatepool_kernel(tc, tab_words, tab_scales, dtab_words, dtab_sc
             gs = slice(h * GH, (h + 1) * GH)
             nc.vector.tensor_tensor(shifted[h][:], by_slot(b[h][:]),
                                     top[:, gs].unsqueeze(1).unsqueeze(3).to_broadcast([P, U, GH, V]), ALU.subtract)
-            nc.scalar.activation(pw[:, :, 0, gs, :], shifted[h][:], ACT.Exp)
-        for h in range(2):
-            gs = slice(h * GH, (h + 1) * GH)
-            nc.vector.tensor_tensor(pw[:, :, 1, gs, :], by_slot(a[:])[:, :, gs, :], pw[:, :, 0, gs, :], ALU.mult)
+            nc.scalar.activation(p[:, :, gs, :], shifted[h][:], ACT.Exp)
 
         dtab_g = [sb.tile([P, HALF], U32, name=f"dtab_g{h}", align_bytes=64) for h in range(2)]
         tb = ps.tile([P, J], F32, name="tb")
@@ -123,20 +120,28 @@ def tile_attend_tcgatepool_kernel(tc, tab_words, tab_scales, dtab_words, dtab_sc
             cols = slice(h * HALF, (h + 1) * HALF)
             product(ta[:, cols], w1q, dtab_g[h][:], dtab_sg[4:P, cols])
 
-        zn = sb.tile([P, 2, G], F32, name="zn", tag="dtab_w", align_bytes=64)
-        nc.vector.tensor_reduce(zn[:], pw[:].rearrange("p u h g v -> p h g u v"), AX.XY, ALU.add)
+        late = sb.tile([P, J + 2 * G], F32, name="late", tag="dtab_w", align_bytes=64)
+        pa = late[:, 0:J].rearrange("p (u g v) -> p u g v", u=U, v=V)
+        z = late[:, J : J + G]
+        n1 = late[:, J + G : J + 2 * G]
+        nc.vector.tensor_tensor(pa, by_slot(a[:]), p[:], ALU.mult)
+        nc.vector.tensor_reduce(z, p[:].rearrange("p u g v -> p g u v"), AX.XY, ALU.add)
 
-        tpw = [sb.tile([P, 2, G, V], F32, name=f"tpw{u}") for u in range(U)]
+        tpw = [sb.tile([P, U // 2, 2, G, V], F32, name=f"tpw{c}") for c in range(2)]
         turned = ps.tile([P, P], F32, name="turned")
-        for u in range(U):
-            nc.vector.tensor_tensor(tpw[u][:], by_slot(tb[:])[:, u].unsqueeze(1).to_broadcast([P, 2, G, V]), pw[:, u], ALU.mult)
-            for v in range(V):
-                nc.tensor.matmul(turned[:], lhsT=tpw[u][:].rearrange("p h g v -> p (h g) v")[:, :, v], rhs=ident[:],
-                                 is_transpose=True, start=(u == 0 and v == 0), stop=(u == U - 1 and v == V - 1))
+        for c in range(2):
+            us = slice(c * U // 2, (c + 1) * U // 2)
+            nc.vector.tensor_tensor(tpw[c][:, :, 0], by_slot(tb[:])[:, us], p[:, us], ALU.mult)
+            nc.vector.tensor_tensor(tpw[c][:, :, 1], by_slot(tb[:])[:, us], pa[:, us], ALU.mult)
+            for u in range(U // 2):
+                for v in range(V):
+                    nc.tensor.matmul(turned[:], lhsT=tpw[c][:, u].rearrange("p h g v -> p (h g) v")[:, :, v], rhs=ident[:],
+                                     is_transpose=True, start=(c == 0 and u == 0 and v == 0),
+                                     stop=(c == 1 and u == U // 2 - 1 and v == V - 1))
         ta_sb = sb.tile([P, U, G, V], F32, name="ta_sb")
         nc.scalar.copy(ta_sb[:], by_slot(ta[:]))
         tap = sb.tile([P, U, G, V], F32, name="tap")
-        nc.gpsimd.tensor_tensor(tap[:], ta_sb[:], pw[:, :, 0], ALU.mult)
+        nc.gpsimd.tensor_tensor(tap[:], ta_sb[:], p[:], ALU.mult)
 
         staged = sb.tile([P, P], F32, name="staged")
         nc.scalar.copy(staged[:], turned[:])
@@ -144,8 +149,9 @@ def tile_attend_tcgatepool_kernel(tc, tab_words, tab_scales, dtab_words, dtab_sc
         nc.tensor.transpose(tzn[:].rearrange("p h g -> p (h g)"), staged[:], ident[:])
 
         rz = sb.tile([P, G], F32, name="rz")
-        nc.vector.reciprocal(rz[:], zn[:, 0, :])
-        nc.vector.scalar_tensor_tensor(coef[:, 0, :], zn[:, 1, :], -1.0, rz[:], ALU.mult, ALU.mult)
+        nc.vector.reciprocal(rz[:], z)
+        nc.vector.tensor_reduce(n1, pa.rearrange("p u g v -> p g u v"), AX.XY, ALU.add)
+        nc.vector.scalar_tensor_tensor(coef[:, 0, :], n1, -1.0, rz[:], ALU.mult, ALU.mult)
         u1 = sb.tile([P, G], F32, name="u1")
         u2 = sb.tile([P, G], F32, name="u2")
         nc.scalar.activation(u1[:], coef[:, 0, :], ACT.Tanh)

@@ -36,8 +36,8 @@ def tile_attend_tcgatepool_kernel(tc, tab_words, tab_scales, dtab_words, dtab_sc
         nc.sync.dma_start(w2_raw[:], w2.rearrange("(p t) r -> p t r", t=PACK))
         tab_sc = sb.tile([P, T], U8, name="tab_sc", align_bytes=64)
         dtab_sc = sb.tile([P, T], U8, name="dtab_sc", align_bytes=64)
-        nc.gpsimd.memset(tab_sc[:].bitcast(I32), 0)
-        nc.gpsimd.memset(dtab_sc[:].bitcast(I32), 0)
+        nc.vector.memset(tab_sc[:].bitcast(I32), 0)
+        nc.vector.memset(dtab_sc[:].bitcast(I32), 0)
         for q in range(4):
             nc.sync.dma_start(tab_sc[32 * q : 32 * q + 4, :].bitcast(I32), tab_scales[0, 4 * q : 4 * q + 4, :].bitcast(I32))
 
@@ -111,14 +111,12 @@ def tile_attend_tcgatepool_kernel(tc, tab_words, tab_scales, dtab_words, dtab_sc
 
         dtab_g = [sb.tile([P, HALF], U32, name=f"dtab_g{h}", align_bytes=64) for h in range(2)]
         tb = ps.tile([P, J], F32, name="tb")
-        ta = ps.tile([P, J], F32, name="ta")
+        ta = [ps.tile([P, HALF], F32, name=f"ta{h}") for h in range(2)]
         for h in range(2):
             cols = slice(h * HALF, (h + 1) * HALF)
             nc.vector.tensor_copy(dtab_g[h][:], dtab_w[:].indirect(list_half(h)))
             product(tb[:, cols], w2q, dtab_g[h][:], dtab_sg[4:P, cols])
-        for h in range(2):
-            cols = slice(h * HALF, (h + 1) * HALF)
-            product(ta[:, cols], w1q, dtab_g[h][:], dtab_sg[4:P, cols])
+            product(ta[h][:], w1q, dtab_g[h][:], dtab_sg[4:P, cols])
 
         late = sb.tile([P, J + 2 * G], F32, name="late", tag="dtab_w", align_bytes=64)
         pa = late[:, 0:J].rearrange("p (u g v) -> p u g v", u=U, v=V)
@@ -127,21 +125,25 @@ def tile_attend_tcgatepool_kernel(tc, tab_words, tab_scales, dtab_words, dtab_sc
         nc.vector.tensor_tensor(pa, by_slot(a[:]), p[:], ALU.mult)
         nc.vector.tensor_reduce(z, p[:].rearrange("p u g v -> p g u v"), AX.XY, ALU.add)
 
-        tpw = [sb.tile([P, U // 2, 2, G, V], F32, name=f"tpw{c}") for c in range(2)]
+        tpw_pair = [sb.tile([P, U // 2, 2, G, V], F32, name=f"tpw_pair{c}") for c in range(2)]
         turned = ps.tile([P, P], F32, name="turned")
         for c in range(2):
             us = slice(c * U // 2, (c + 1) * U // 2)
-            nc.vector.tensor_tensor(tpw[c][:, :, 0], by_slot(tb[:])[:, us], p[:, us], ALU.mult)
-            nc.vector.tensor_tensor(tpw[c][:, :, 1], by_slot(tb[:])[:, us], pa[:, us], ALU.mult)
-            for u in range(U // 2):
-                for v in range(V):
-                    nc.tensor.matmul(turned[:], lhsT=tpw[c][:, u].rearrange("p h g v -> p (h g) v")[:, :, v], rhs=ident[:],
-                                     is_transpose=True, start=(c == 0 and u == 0 and v == 0),
-                                     stop=(c == 1 and u == U // 2 - 1 and v == V - 1))
-        ta_sb = sb.tile([P, U, G, V], F32, name="ta_sb")
-        nc.scalar.copy(ta_sb[:], by_slot(ta[:]))
+            nc.vector.tensor_tensor(tpw_pair[c][:, :, 0], by_slot(tb[:])[:, us], p[:, us], ALU.mult)
+            pieces = [(0, 2)] if c == 0 else [(0, 1), (1, 2)]
+            for lo, hi in pieces:
+                nc.vector.tensor_tensor(tpw_pair[c][:, lo:hi, 1], by_slot(tb[:])[:, 2 * c + lo : 2 * c + hi], pa[:, 2 * c + lo : 2 * c + hi], ALU.mult)
+                for u in range(lo, hi):
+                    for v in range(V):
+                        nc.tensor.matmul(turned[:], lhsT=tpw_pair[c][:, u].rearrange("p h g v -> p (h g) v")[:, :, v], rhs=ident[:],
+                                         is_transpose=True, start=(c == 0 and u == 0 and v == 0),
+                                         stop=(c == 1 and u == U // 2 - 1 and v == V - 1))
         tap = sb.tile([P, U, G, V], F32, name="tap")
-        nc.gpsimd.tensor_tensor(tap[:], ta_sb[:], p[:], ALU.mult)
+        for h in range(2):
+            gs = slice(h * GH, (h + 1) * GH)
+            ta_sb = sb.tile([P, U, GH, V], F32, name=f"ta_sb{h}")
+            nc.scalar.copy(ta_sb[:], by_slot(ta[h][:]))
+            nc.gpsimd.tensor_tensor(tap[:, :, gs, :], ta_sb[:], p[:, :, gs, :], ALU.mult)
 
         staged = sb.tile([P, P], F32, name="staged")
         nc.scalar.copy(staged[:], turned[:])

from contextlib import ExitStack

import concourse.mybir as mybir
from concourse.masks import make_identity

K, R, T, J, G = 512, 128, 2048, 512, 64
P = 128
PACK = 4
U, V = 4, 2
HALF = J // 2
GH = G // 2
FLOPS = 4 * 2 * K * R * J

F32 = mybir.dt.float32
BF16 = mybir.dt.bfloat16
I32 = mybir.dt.int32
U32 = mybir.dt.uint32
U16 = mybir.dt.uint16
U8 = mybir.dt.uint8
FP8X4 = mybir.dt.float8_e4m3fn_x4
ALU = mybir.AluOpType
ACT = mybir.ActivationFunctionType
AX = mybir.AxisListType


def tile_attend_tcgatepool_kernel(tc, tab_words, tab_scales, dtab_words, dtab_scales, w1, w2, og, base, offs, out):
    nc = tc.nc
    with ExitStack() as ctx:
        sb = ctx.enter_context(tc.tile_pool(name="sb", bufs=1))
        ps = ctx.enter_context(tc.psum_pool(name="ps", bufs=1))

        offsets = sb.tile([P, J // 16], U16, name="offsets")
        nc.sync.dma_start(offsets[:], offs)

        w2_raw = sb.tile([P, PACK, R], F32, name="w2_raw")
        nc.sync.dma_start(w2_raw[:], w2.rearrange("(p t) r -> p t r", t=PACK))
        tab_sc = sb.tile([P, T], U8, name="tab_sc", align_bytes=64)
        dtab_sc = sb.tile([P, T], U8, name="dtab_sc", align_bytes=64)
        nc.vector.memset(tab_sc[:].bitcast(I32), 0)
        nc.vector.memset(dtab_sc[:].bitcast(I32), 0)
        for q in range(4):
            nc.sync.dma_start(tab_sc[32 * q : 32 * q + 4, :].bitcast(I32), tab_scales[0, 4 * q : 4 * q + 4, :].bitcast(I32))

        w1_raw = sb.tile([P, PACK, R], F32, name="w1_raw")
        tab_w = sb.tile([P, T], U32, name="tab_w", align_bytes=64)
        dtab_w = sb.tile([P, T], U32, name="dtab_w", align_bytes=64)
        nc.sync.dma_start(tab_w[:].bitcast(I32), tab_words[0].rearrange("p n t -> p (n t)").bitcast(I32))
        for q in range(4):
            nc.sync.dma_start(dtab_sc[32 * q + 4 : 32 * q + 8, :].bitcast(I32), dtab_scales[0, 4 * q : 4 * q + 4, :].bitcast(I32))
        nc.sync.dma_start(w1_raw[:], w1.rearrange("(p t) r -> p t r", t=PACK))
        nc.sync.dma_start(dtab_w[:].bitcast(I32), dtab_words[0].rearrange("p n t -> p (n t)").bitcast(I32))

        ident = sb.tile([P, P], F32, name="ident")
        make_identity(nc, ident[:])
        warm = sb.tile([P, 1], F32, name="warm")
        nc.scalar.activation(warm[:], ident[:, 0:1], ACT.Exp)
        gain = sb.tile([P, 1], F32, name="gain")
        nc.gpsimd.dma_start(gain[:], og)
        base_sb = sb.tile([P, G], F32, name="base_sb")
        nc.gpsimd.dma_start(base_sb[:], base)
        neg_gain = sb.tile([P, 1], F32, name="neg_gain")
        nc.gpsimd.tensor_scalar(neg_gain[:], gain[:], -1.0, 0.0, ALU.mult, ALU.add)
        coef = sb.tile([P, 2, G], F32, name="coef")
        nc.gpsimd.memset(coef[:, 1, :], 1.0)

        tab_sg = sb.tile([P, J], U8, name="tab_sg", align_bytes=64)
        dtab_sg = sb.tile([P, J], U8, name="dtab_sg", align_bytes=64)
        nc.vector.tensor_copy(tab_sg[:], tab_sc[:].indirect(offsets[:]))

        def quantise(raw, name):
            grouped = sb.tile([P, R, PACK], BF16, name=name + "_grouped", align_bytes=64)
            nc.scalar.copy(grouped[:], raw[:].rearrange("p t r -> p r t"))
            codes = sb.tile([P, R], U32, name=name + "_codes", align_bytes=64)
            scales = sb.tile([P, R], U8, name=name + "_scales", align_bytes=64)
            nc.vector.quantize_mx(out=codes[:].bitcast(FP8X4), scales=scales[:], in_=grouped[:].rearrange("p r t -> p (r t)"))
            return codes, scales

        def product(dst, weights, words, scales):
            nc.tensor.matmul_mx(out=dst, lhsT=weights[0][:].bitcast(FP8X4), lhsT_scale=weights[1][:],
                                rhs=words.bitcast(FP8X4), rhs_scale=scales, start=True, stop=True)

        def list_half(h):
            return offsets[:, h * (HALF // 16) : (h + 1) * (HALF // 16)]

        def by_slot(bank):
            return bank.rearrange("p (g u v) -> p u g v", u=U, v=V)

        w2q = quantise(w2_raw, "w2")
        tab_g = [sb.tile([P, HALF], U32, name=f"tab_g{h}", align_bytes=64) for h in range(2)]
        b = [ps.tile([P, HALF], F32, name=f"b{h}") for h in range(2)]
        a = ps.tile([P, J], F32, name="a")
        for h in range(2):
            nc.vector.tensor_copy(tab_g[h][:], tab_w[:].indirect(list_half(h)))
            product(b[h][:], w2q, tab_g[h][:], tab_sg[:, h * HALF : (h + 1) * HALF])
        nc.vector.tensor_copy(dtab_sg[:], dtab_sc[:].indirect(offsets[:]))
        w1q = quantise(w1_raw, "w1")
        for h in range(2):
            product(a[:, h * HALF : (h + 1) * HALF], w1q, tab_g[h][:], tab_sg[:, h * HALF : (h + 1) * HALF])

        top = sb.tile([P, G], F32, name="top", tag="dtab_sc", align_bytes=64)
        shifted = [sb.tile([P, U, GH, V], F32, name=f"shifted{h}") for h in range(2)]
        p = sb.tile([P, U, G, V], F32, name="p")
        for h in range(2):
            gs = slice(h * GH, (h + 1) * GH)
            nc.vector.tensor_reduce(top[:, gs], b[h][:].rearrange("p (g i) -> p g i", i=U * V), AX.X, ALU.max)
        for h in range(2):
            gs = slice(h * GH, (h + 1) * GH)
            nc.vector.tensor_tensor(shifted[h][:], by_slot(b[h][:]),
                                    top[:, gs].unsqueeze(1).unsqueeze(3).to_broadcast([P, U, GH, V]), ALU.subtract)
            nc.scalar.activation(p[:, :, gs, :], shifted[h][:], ACT.Exp)

        dtab_g = [sb.tile([P, HALF], U32, name=f"dtab_g{h}", align_bytes=64) for h in range(2)]
        tb = ps.tile([P, J], F32, name="tb")
        ta = [ps.tile([P, HALF], F32, name=f"ta{h}") for h in range(2)]
        for h in range(2):
            cols = slice(h * HALF, (h + 1) * HALF)
            nc.vector.tensor_copy(dtab_g[h][:], dtab_w[:].indirect(list_half(h)))
            product(tb[:, cols], w2q, dtab_g[h][:], dtab_sg[4:P, cols])
            product(ta[h][:], w1q, dtab_g[h][:], dtab_sg[4:P, cols])

        late = sb.tile([P, J + 2 * G], F32, name="late", tag="dtab_w", align_bytes=64)
        pa = late[:, 0:J].rearrange("p (u g v) -> p u g v", u=U, v=V)
        z = late[:, J : J + G]
        n1 = late[:, J + G : J + 2 * G]
        nc.vector.tensor_tensor(pa, by_slot(a[:]), p[:], ALU.mult)
        nc.vector.tensor_reduce(z, p[:].rearrange("p u g v -> p g u v"), AX.XY, ALU.add)

        tpw_pair = [sb.tile([P, U // 2, 2, G, V], F32, name=f"tpw_pair{c}") for c in range(2)]
        turned = ps.tile([P, P], F32, name="turned")
        for c in range(2):
            us = slice(c * U // 2, (c + 1) * U // 2)
            nc.vector.tensor_tensor(tpw_pair[c][:, :, 0], by_slot(tb[:])[:, us], p[:, us], ALU.mult)
            pieces = [(0, 2)] if c == 0 else [(0, 1), (1, 2)]
            for lo, hi in pieces:
                nc.vector.tensor_tensor(tpw_pair[c][:, lo:hi, 1], by_slot(tb[:])[:, 2 * c + lo : 2 * c + hi], pa[:, 2 * c + lo : 2 * c + hi], ALU.mult)
                for u in range(lo, hi):
                    for v in range(V):
                        nc.tensor.matmul(turned[:], lhsT=tpw_pair[c][:, u].rearrange("p h g v -> p (h g) v")[:, :, v], rhs=ident[:],
                                         is_transpose=True, start=(c == 0 and u == 0 and v == 0),
                                         stop=(c == 1 and u == U // 2 - 1 and v == V - 1))
        tap = sb.tile([P, U, G, V], F32, name="tap")
        for h in range(2):
            gs = slice(h * GH, (h + 1) * GH)
            ta_sb = sb.tile([P, U, GH, V], F32, name=f"ta_sb{h}")
            nc.scalar.copy(ta_sb[:], by_slot(ta[h][:]))
            nc.gpsimd.tensor_tensor(tap[:, :, gs, :], ta_sb[:], p[:, :, gs, :], ALU.mult)

        staged = sb.tile([P, P], F32, name="staged")
        nc.scalar.copy(staged[:], turned[:])
        tzn = ps.tile([P, 2, G], F32, name="tzn")
        nc.tensor.transpose(tzn[:].rearrange("p h g -> p (h g)"), staged[:], ident[:])

        rz = sb.tile([P, G], F32, name="rz")
        nc.vector.reciprocal(rz[:], z)
        nc.vector.tensor_reduce(n1, pa.rearrange("p u g v -> p g u v"), AX.XY, ALU.add)
        nc.vector.scalar_tensor_tensor(coef[:, 0, :], n1, -1.0, rz[:], ALU.mult, ALU.mult)
        u1 = sb.tile([P, G], F32, name="u1")
        u2 = sb.tile([P, G], F32, name="u2")
        nc.scalar.activation(u1[:], coef[:, 0, :], ACT.Tanh)
        nc.scalar.activation(u2[:], u1[:], ACT.Square)

        terms = sb.tile([P, 3, G], F32, name="terms")
        nc.vector.tensor_reduce(terms[:, 2, :], tap[:].rearrange("p u g v -> p g u v"), AX.XY, ALU.add)
        nc.vector.tensor_tensor(terms[:, 0:2, :], tzn[:], coef[:], ALU.mult)
        slope = sb.tile([P, G], F32, name="slope")
        nc.vector.scalar_tensor_tensor(slope[:], u2[:], 1.0, rz[:], ALU.subtract, ALU.mult)
        total = sb.tile([P, G], F32, name="total")
        nc.vector.tensor_reduce(total[:], terms[:].rearrange("p s g -> p g s"), AX.X, ALU.add)
        scaled = sb.tile([P, G], F32, name="scaled")
        nc.vector.scalar_tensor_tensor(scaled[:], total[:], neg_gain[:], slope[:], ALU.mult, ALU.mult)
        res = sb.tile([P, G], F32, name="res")
        nc.vector.tensor_tensor(res[:], scaled[:], base_sb[:], ALU.add)
        nc.sync.dma_start(out, res[:])
